import numpy as np
import ml_dtypes


def mxq(x, axis, fmt="e4m3"):
    dtype, down = {"e4m3": (ml_dtypes.float8_e4m3fn, 7), "e5m2": (ml_dtypes.float8_e5m2, 14)}[fmt]
    v = np.moveaxis(np.asarray(x, np.float32).astype(ml_dtypes.bfloat16).astype(np.float64), axis, -1)
    blocks = v.reshape(v.shape[:-1] + (-1, 32))
    amax = np.abs(blocks).max(-1, keepdims=True)
    byte = np.maximum(np.where(amax > 0, np.frexp(amax)[1] - 1 + 127, 0) - down, 1)
    scale = np.exp2(byte - 127.0)
    codes = (blocks / scale).astype(np.float32).astype(dtype).astype(np.float64)
    return np.moveaxis((codes * scale).reshape(v.shape), -1, axis)


WIDE = False


def mx_kscale(k):
    if not WIDE:
        return np.ones(k)
    levels = np.array([10, -10, 5, -5, 0])
    if k % 512:
        return np.exp2(np.random.permutation(np.resize(levels, k // 32))).repeat(32)
    a = np.empty((k // 512, 16))
    for p in range(k // 512):
        a[p, :8] = np.random.permutation(np.resize(levels, 8))
        for g in range(8):
            far = levels[np.abs(levels - a[p, g]) >= 10]
            a[p, g + 8] = far[np.random.randint(len(far))]
    return np.exp2(a.ravel()).repeat(32)


def f64(x):
    return np.asarray(x).astype(np.float64)


def striped(idx):
    return np.tile(idx.reshape(-1, 16).T, (8, 1)).astype(np.uint16)


def unstriped(offs):
    return offs[:16].T.reshape(-1).astype(np.int64)


K, T, S, N = 512, 2048, 512, 128


def setup_inputs():
    n = np.random.standard_normal
    s = mx_kscale(K)[:, None]
    return {
        "xT": (n((K, T)) * s).astype(np.float32),
        "w1": (n((K, N)) / np.sqrt(K) / s).astype(np.float32),
        "offs": striped(np.random.permutation(T)[:S]),
    }


def reference(xT, w1, offs):
    xq = mxq(f64(xT)[:, unstriped(offs)], 0, "e4m3")
    y = mxq(f64(w1), 0, "e4m3").T @ xq
    e = np.exp(y - y.max(axis=1, keepdims=True))
    return e / e.sum(axis=1, keepdims=True)

@@ -1,0 +1,105 @@
+from contextlib import ExitStack
+
+import concourse.mybir as mybir
+
+K, T, S, N = 512, 2048, 512, 128
+FLOPS = 2 * K * S * N
+
+F32 = mybir.dt.float32
+BF16 = mybir.dt.bfloat16
+U32 = mybir.dt.uint32
+U16 = mybir.dt.uint16
+U8 = mybir.dt.uint8
+FP8X4 = mybir.dt.float8_e4m3fn_x4
+ALU = mybir.AluOpType
+ACT = mybir.ActivationFunctionType
+
+P = 128
+PACK = 4
+HALF = S // 2
+
+
+def tile_picked_rank_none_e_kernel(tc, xT, w1, offs, out):
+    nc = tc.nc
+    with ExitStack() as ctx:
+        keep = ctx.enter_context(tc.tile_pool(name="keep", bufs=1))
+        psum = ctx.enter_context(tc.psum_pool(name="psum", bufs=1))
+
+        offsets = keep.tile([P, S // 16], U16, name="offsets")
+        nc.sync.dma_start(offsets[:], offs)
+
+        x_rows = xT.rearrange("(p j) t -> p j t", j=PACK)
+        planes = [keep.tile([P, T], F32, name=f"plane{j}") for j in range(PACK)]
+        for j in range(PACK):
+            nc.sync.dma_start(out=planes[j][:], in_=x_rows[:, j, :])
+        w_raw = keep.tile([P, PACK, N], F32, name="w_raw")
+        nc.sync.dma_start(out=w_raw[:], in_=w1.rearrange("(p j) m -> p j m", j=PACK))
+
+        warm_in = keep.tile([P, 1], F32, name="warm_in")
+        warm_out = keep.tile([P, 1], F32, name="warm_out")
+        nc.vector.memset(warm_in[:], 0.0)
+        nc.scalar.activation(out=warm_out[:], in_=warm_in[:], func=ACT.Exp)
+
+        woven = [keep.tile([P, HALF, PACK], BF16, name=f"woven{h}", align_bytes=64) for h in range(2)]
+        for j in range(PACK):
+            for h in range(2):
+                cols = offsets[:, h * HALF // 16 : (h + 1) * HALF // 16]
+                nc.vector.tensor_copy(woven[h][:, :, j], planes[j][:].indirect(cols))
+
+        w_woven = keep.tile([P, N, PACK], BF16, name="w_woven", align_bytes=64)
+        nc.scalar.copy(
+            out=w_woven[:].rearrange("p (c i) j -> p c j i", i=4),
+            in_=w_raw[:].rearrange("p j (c i) -> p c j i", i=4),
+        )
+        w_codes = keep.tile([P, N], U32, name="w_codes", align_bytes=64)
+        w_scales = keep.tile([P, N], U8, name="w_scales", align_bytes=64)
+        nc.vector.quantize_mx(
+            out=w_codes[:].bitcast(FP8X4), scales=w_scales[:], in_=w_woven[:].rearrange("p m j -> p (m j)")
+        )
+
+        x_codes = [keep.tile([P, HALF], U32, name=f"x_codes{h}", align_bytes=64) for h in range(2)]
+        x_scales = [keep.tile([P, HALF], U8, name=f"x_scales{h}", align_bytes=64) for h in range(2)]
+        scores = [psum.tile([P, HALF], F32, name=f"scores{h}") for h in range(2)]
+        for h in range(2):
+            nc.vector.quantize_mx(
+                out=x_codes[h][:].bitcast(FP8X4),
+                scales=x_scales[h][:],
+                in_=woven[h][:].rearrange("p c j -> p (c j)"),
+            )
+            nc.tensor.matmul_mx(
+                out=scores[h][:],
+                lhsT=w_codes[:].bitcast(FP8X4),
+                lhsT_scale=w_scales[:],
+                rhs=x_codes[h][:].bitcast(FP8X4),
+                rhs_scale=x_scales[h][:],
+                start=True,
+                stop=True,
+            )
+
+        neg_scores = keep.tile([P, S], F32, name="neg_scores")
+        neg_max = [keep.tile([P, 1], F32, name=f"neg_max{h}") for h in range(2)]
+        for h in range(2):
+            nc.vector.tensor_scalar(
+                out=neg_scores[:, h * HALF : (h + 1) * HALF],
+                in0=scores[h][:],
+                scalar1=-1.0,
+                scalar2=(neg_max[0][:] if h else None),
+                op0=ALU.mult,
+                op1=ALU.min,
+                accum_out=neg_max[h][:],
+            )
+
+        exps = keep.tile([P, S], F32, name="exps")
+        total = keep.tile([P, 1], F32, name="total")
+        nc.scalar.activation(
+            out=exps[:], in_=neg_scores[:], func=ACT.Exp, bias=neg_max[1][:], scale=-1.0, accum_out=total[:]
+        )
+        inv_total = keep.tile([P, 1], F32, name="inv_total")
+        nc.vector.reciprocal(out=inv_total[:], in_=total[:])
+        result = [keep.tile([P, HALF], F32, name=f"result{h}") for h in range(2)]
+        for h, queue in enumerate((nc.sync, nc.scalar)):
+            cols = slice(h * HALF, (h + 1) * HALF)
+            nc.vector.tensor_scalar(
+                out=result[h][:], in0=exps[:, cols], scalar1=inv_total[:], scalar2=None, op0=ALU.mult
+            )
+            queue.dma_start(out=out[:, cols], in_=result[h][:])

@@ -17,6 +17,8 @@ ACT = mybir.ActivationFunctionType
 P = 128
 PACK = 4
 HALF = S // 2
+CHUNKS = ((0, 512), (512, 1280), (1280, 1792), (1792, 2048))
+VECTOR_CHUNK = 2
 
 
 def tile_picked_rank_none_e_kernel(tc, xT, w1, offs, out):
@@ -26,13 +28,16 @@ def tile_picked_rank_none_e_kernel(tc, xT, w1, offs, out):
         psum = ctx.enter_context(tc.psum_pool(name="psum", bufs=1))
 
         offsets = keep.tile([P, S // 16], U16, name="offsets")
-        nc.sync.dma_start(offsets[:], offs)
 
         x_rows = xT.rearrange("(p j) t -> p j t", j=PACK)
         planes = [keep.tile([P, T], F32, name=f"plane{j}") for j in range(PACK)]
-        for j in range(PACK):
+        nc.sync.dma_start(out=planes[2][:], in_=x_rows[:, 2, :])
+        nc.sync.dma_start(offsets[:], offs)
+        for j in (0, 1):
             nc.sync.dma_start(out=planes[j][:], in_=x_rows[:, j, :])
-        w_raw = keep.tile([P, PACK, N], F32, name="w_raw")
+        for lo, hi in CHUNKS:
+            nc.sync.dma_start(out=planes[3][:, lo:hi], in_=x_rows[:, 3, lo:hi])
+        w_raw = keep.tile([P, PACK, N], F32, name="w_raw", tag="slot0", align_bytes=64)
         nc.sync.dma_start(out=w_raw[:], in_=w1.rearrange("(p j) m -> p j m", j=PACK))
 
         warm_in = keep.tile([P, 1], F32, name="warm_in")
@@ -41,13 +46,25 @@ def tile_picked_rank_none_e_kernel(tc, xT, w1, offs, out):
         nc.scalar.activation(out=warm_out[:], in_=warm_in[:], func=ACT.Exp)
 
         woven = [keep.tile([P, HALF, PACK], BF16, name=f"woven{h}", align_bytes=64) for h in range(2)]
-        for j in range(PACK):
-            for h in range(2):
-                cols = offsets[:, h * HALF // 16 : (h + 1) * HALF // 16]
-                nc.vector.tensor_copy(woven[h][:, :, j], planes[j][:].indirect(cols))
+        lists = [offsets[:, h * HALF // 16 : (h + 1) * HALF // 16] for h in range(2)]
+        rounded = {j: keep.tile([P, T], BF16, name=f"rounded{j}") for j in (2, 3)}
 
-        w_woven = keep.tile([P, N, PACK], BF16, name="w_woven", align_bytes=64)
-        nc.scalar.copy(
+        nc.vector.tensor_copy(woven[0][:, :, 2], planes[2][:].indirect(lists[0]))
+        nc.scalar.activation(out=rounded[2][:], in_=planes[2][:], func=ACT.Copy)
+        nc.scalar.activation(out=woven[1][:, :, 2], in_=rounded[2][:].indirect(lists[1]), func=ACT.Copy)
+        for j in (0, 1):
+            for h in range(2):
+                nc.vector.tensor_copy(woven[h][:, :, j], planes[j][:].indirect(lists[h]))
+        for c, (lo, hi) in enumerate(CHUNKS):
+            if c == VECTOR_CHUNK:
+                nc.vector.tensor_copy(rounded[3][:, lo:hi], planes[3][:, lo:hi])
+            else:
+                nc.scalar.activation(out=rounded[3][:, lo:hi], in_=planes[3][:, lo:hi], func=ACT.Copy)
+        nc.vector.tensor_copy(woven[0][:, :, 3], planes[3][:].indirect(lists[0]))
+        nc.scalar.activation(out=woven[1][:, :, 3], in_=rounded[3][:].indirect(lists[1]), func=ACT.Copy)
+
+        w_woven = keep.tile([P, N, PACK], BF16, name="w_woven", tag="slot1", align_bytes=64)
+        nc.vector.tensor_copy(
             out=w_woven[:].rearrange("p (c i) j -> p c j i", i=4),
             in_=w_raw[:].rearrange("p j (c i) -> p c j i", i=4),
         )
@@ -57,7 +74,7 @@ def tile_picked_rank_none_e_kernel(tc, xT, w1, offs, out):
             out=w_codes[:].bitcast(FP8X4), scales=w_scales[:], in_=w_woven[:].rearrange("p m j -> p (m j)")
         )
 
-        x_codes = [keep.tile([P, HALF], U32, name=f"x_codes{h}", align_bytes=64) for h in range(2)]
+        x_codes = [keep.tile([P, HALF], U32, name=f"x_codes{h}", tag=f"slot{h}", align_bytes=64) for h in range(2)]
         x_scales = [keep.tile([P, HALF], U8, name=f"x_scales{h}", align_bytes=64) for h in range(2)]
         scores = [psum.tile([P, HALF], F32, name=f"scores{h}") for h in range(2)]
         for h in range(2):

@@ -17,8 +17,9 @@ ACT = mybir.ActivationFunctionType
 P = 128
 PACK = 4
 HALF = S // 2
-CHUNKS = ((0, 512), (512, 1280), (1280, 1792), (1792, 2048))
-VECTOR_CHUNK = 2
+CHUNKS = ((0, 1280), (1280, 1792), (1792, 2048))
+SCALAR_CASTS = ((0, 768), (1792, 2048))
+VECTOR_CASTS = ((768, 1280), (1280, 1792))
 
 
 def tile_picked_rank_none_e_kernel(tc, xT, w1, offs, out):
@@ -40,11 +41,6 @@ def tile_picked_rank_none_e_kernel(tc, xT, w1, offs, out):
         w_raw = keep.tile([P, PACK, N], F32, name="w_raw", tag="slot0", align_bytes=64)
         nc.sync.dma_start(out=w_raw[:], in_=w1.rearrange("(p j) m -> p j m", j=PACK))
 
-        warm_in = keep.tile([P, 1], F32, name="warm_in")
-        warm_out = keep.tile([P, 1], F32, name="warm_out")
-        nc.vector.memset(warm_in[:], 0.0)
-        nc.scalar.activation(out=warm_out[:], in_=warm_in[:], func=ACT.Exp)
-
         woven = [keep.tile([P, HALF, PACK], BF16, name=f"woven{h}", align_bytes=64) for h in range(2)]
         lists = [offsets[:, h * HALF // 16 : (h + 1) * HALF // 16] for h in range(2)]
         rounded = {j: keep.tile([P, T], BF16, name=f"rounded{j}") for j in (2, 3)}
@@ -55,11 +51,10 @@ def tile_picked_rank_none_e_kernel(tc, xT, w1, offs, out):
         for j in (0, 1):
             for h in range(2):
                 nc.vector.tensor_copy(woven[h][:, :, j], planes[j][:].indirect(lists[h]))
-        for c, (lo, hi) in enumerate(CHUNKS):
-            if c == VECTOR_CHUNK:
-                nc.vector.tensor_copy(rounded[3][:, lo:hi], planes[3][:, lo:hi])
-            else:
-                nc.scalar.activation(out=rounded[3][:, lo:hi], in_=planes[3][:, lo:hi], func=ACT.Copy)
+        for lo, hi in VECTOR_CASTS:
+            nc.vector.tensor_copy(rounded[3][:, lo:hi], planes[3][:, lo:hi])
+        for lo, hi in SCALAR_CASTS:
+            nc.scalar.activation(out=rounded[3][:, lo:hi], in_=planes[3][:, lo:hi], func=ACT.Copy)
         nc.vector.tensor_copy(woven[0][:, :, 3], planes[3][:].indirect(lists[0]))
         nc.scalar.activation(out=woven[1][:, :, 3], in_=rounded[3][:].indirect(lists[1]), func=ACT.Copy)
 
@@ -76,28 +71,34 @@ def tile_picked_rank_none_e_kernel(tc, xT, w1, offs, out):
 
         x_codes = [keep.tile([P, HALF], U32, name=f"x_codes{h}", tag=f"slot{h}", align_bytes=64) for h in range(2)]
         x_scales = [keep.tile([P, HALF], U8, name=f"x_scales{h}", align_bytes=64) for h in range(2)]
-        scores = [psum.tile([P, HALF], F32, name=f"scores{h}") for h in range(2)]
+        FIRST = 128
+        scores = [psum.tile([P, w], F32, name=f"scores{b}") for b, w in enumerate((FIRST, S - FIRST))]
+        pieces = (
+            ((0, FIRST, scores[0][:]), (FIRST, HALF, scores[1][:, : HALF - FIRST])),
+            ((0, HALF, scores[1][:, HALF - FIRST :]),),
+        )
         for h in range(2):
             nc.vector.quantize_mx(
                 out=x_codes[h][:].bitcast(FP8X4),
                 scales=x_scales[h][:],
                 in_=woven[h][:].rearrange("p c j -> p (c j)"),
             )
-            nc.tensor.matmul_mx(
-                out=scores[h][:],
-                lhsT=w_codes[:].bitcast(FP8X4),
-                lhsT_scale=w_scales[:],
-                rhs=x_codes[h][:].bitcast(FP8X4),
-                rhs_scale=x_scales[h][:],
-                start=True,
-                stop=True,
-            )
+            for lo, hi, dst in pieces[h]:
+                nc.tensor.matmul_mx(
+                    out=dst,
+                    lhsT=w_codes[:].bitcast(FP8X4),
+                    lhsT_scale=w_scales[:],
+                    rhs=x_codes[h][:, lo:hi].bitcast(FP8X4),
+                    rhs_scale=x_scales[h][:, lo:hi],
+                    start=True,
+                    stop=True,
+                )
 
         neg_scores = keep.tile([P, S], F32, name="neg_scores")
         neg_max = [keep.tile([P, 1], F32, name=f"neg_max{h}") for h in range(2)]
-        for h in range(2):
+        for h, cols in enumerate((slice(0, FIRST), slice(FIRST, S))):
             nc.vector.tensor_scalar(
-                out=neg_scores[:, h * HALF : (h + 1) * HALF],
+                out=neg_scores[:, cols],
                 in0=scores[h][:],
                 scalar1=-1.0,
                 scalar2=(neg_max[0][:] if h else None),

@@ -17,9 +17,9 @@ ACT = mybir.ActivationFunctionType
 P = 128
 PACK = 4
 HALF = S // 2
-CHUNKS = ((0, 1280), (1280, 1792), (1792, 2048))
-SCALAR_CASTS = ((0, 768), (1792, 2048))
-VECTOR_CASTS = ((768, 1280), (1280, 1792))
+CHUNKS = ((0, 704), (704, 1408), (1408, 1792), (1792, 2048))
+SCALAR_CASTS = ((0, 704), (704, 1408), (1792, 2048))
+VECTOR_CASTS = ((1408, 1792),)
 
 
 def tile_picked_rank_none_e_kernel(tc, xT, w1, offs, out):
@@ -41,7 +41,9 @@ def tile_picked_rank_none_e_kernel(tc, xT, w1, offs, out):
         w_raw = keep.tile([P, PACK, N], F32, name="w_raw", tag="slot0", align_bytes=64)
         nc.sync.dma_start(out=w_raw[:], in_=w1.rearrange("(p j) m -> p j m", j=PACK))
 
-        woven = [keep.tile([P, HALF, PACK], BF16, name=f"woven{h}", align_bytes=64) for h in range(2)]
+        woven_flat = keep.tile([P, S * PACK], BF16, name="woven_flat", align_bytes=64)
+        woven_all = woven_flat[:].rearrange("p (c j) -> p c j", j=PACK)
+        woven = [woven_all[:, h * HALF : (h + 1) * HALF, :] for h in range(2)]
         lists = [offsets[:, h * HALF // 16 : (h + 1) * HALF // 16] for h in range(2)]
         rounded = {j: keep.tile([P, T], BF16, name=f"rounded{j}") for j in (2, 3)}
 
@@ -49,8 +51,7 @@ def tile_picked_rank_none_e_kernel(tc, xT, w1, offs, out):
         nc.scalar.activation(out=rounded[2][:], in_=planes[2][:], func=ACT.Copy)
         nc.scalar.activation(out=woven[1][:, :, 2], in_=rounded[2][:].indirect(lists[1]), func=ACT.Copy)
         for j in (0, 1):
-            for h in range(2):
-                nc.vector.tensor_copy(woven[h][:, :, j], planes[j][:].indirect(lists[h]))
+            nc.vector.tensor_copy(woven_all[:, :, j], planes[j][:].indirect(offsets[:]))
         for lo, hi in VECTOR_CASTS:
             nc.vector.tensor_copy(rounded[3][:, lo:hi], planes[3][:, lo:hi])
         for lo, hi in SCALAR_CASTS:
@@ -81,7 +82,7 @@ def tile_picked_rank_none_e_kernel(tc, xT, w1, offs, out):
             nc.vector.quantize_mx(
                 out=x_codes[h][:].bitcast(FP8X4),
                 scales=x_scales[h][:],
-                in_=woven[h][:].rearrange("p c j -> p (c j)"),
+                in_=woven_flat[:, h * HALF * PACK : (h + 1) * HALF * PACK],
             )
             for lo, hi, dst in pieces[h]:
                 nc.tensor.matmul_mx(

from contextlib import ExitStack

import concourse.mybir as mybir

K, T, S, N = 512, 2048, 512, 128
FLOPS = 2 * K * S * N

F32 = mybir.dt.float32
BF16 = mybir.dt.bfloat16
U32 = mybir.dt.uint32
U16 = mybir.dt.uint16
U8 = mybir.dt.uint8
FP8X4 = mybir.dt.float8_e4m3fn_x4
ALU = mybir.AluOpType
ACT = mybir.ActivationFunctionType

P = 128
PACK = 4
HALF = S // 2
CHUNKS = ((0, 704), (704, 1408), (1408, 1792), (1792, 2048))
SCALAR_CASTS = ((0, 704), (704, 1408), (1792, 2048))
VECTOR_CASTS = ((1408, 1792),)


def tile_picked_rank_none_e_kernel(tc, xT, w1, offs, out):
    nc = tc.nc
    with ExitStack() as ctx:
        keep = ctx.enter_context(tc.tile_pool(name="keep", bufs=1))
        psum = ctx.enter_context(tc.psum_pool(name="psum", bufs=1))

        offsets = keep.tile([P, S // 16], U16, name="offsets")

        x_rows = xT.rearrange("(p j) t -> p j t", j=PACK)
        planes = [keep.tile([P, T], F32, name=f"plane{j}") for j in range(PACK)]
        nc.sync.dma_start(out=planes[2][:], in_=x_rows[:, 2, :])
        nc.sync.dma_start(offsets[:], offs)
        for j in (0, 1):
            nc.sync.dma_start(out=planes[j][:], in_=x_rows[:, j, :])
        for lo, hi in CHUNKS:
            nc.sync.dma_start(out=planes[3][:, lo:hi], in_=x_rows[:, 3, lo:hi])
        w_raw = keep.tile([P, PACK, N], F32, name="w_raw", tag="slot0", align_bytes=64)
        nc.sync.dma_start(out=w_raw[:], in_=w1.rearrange("(p j) m -> p j m", j=PACK))

        woven_flat = keep.tile([P, S * PACK], BF16, name="woven_flat", align_bytes=64)
        woven_all = woven_flat[:].rearrange("p (c j) -> p c j", j=PACK)
        woven = [woven_all[:, h * HALF : (h + 1) * HALF, :] for h in range(2)]
        lists = [offsets[:, h * HALF // 16 : (h + 1) * HALF // 16] for h in range(2)]
        rounded = {j: keep.tile([P, T], BF16, name=f"rounded{j}") for j in (2, 3)}

        nc.vector.tensor_copy(woven[0][:, :, 2], planes[2][:].indirect(lists[0]))
        nc.scalar.activation(out=rounded[2][:], in_=planes[2][:], func=ACT.Copy)
        nc.scalar.activation(out=woven[1][:, :, 2], in_=rounded[2][:].indirect(lists[1]), func=ACT.Copy)
        for j in (0, 1):
            nc.vector.tensor_copy(woven_all[:, :, j], planes[j][:].indirect(offsets[:]))
        for lo, hi in VECTOR_CASTS:
            nc.vector.tensor_copy(rounded[3][:, lo:hi], planes[3][:, lo:hi])
        for lo, hi in SCALAR_CASTS:
            nc.scalar.activation(out=rounded[3][:, lo:hi], in_=planes[3][:, lo:hi], func=ACT.Copy)
        nc.vector.tensor_copy(woven[0][:, :, 3], planes[3][:].indirect(lists[0]))
        nc.scalar.activation(out=woven[1][:, :, 3], in_=rounded[3][:].indirect(lists[1]), func=ACT.Copy)

        w_woven = keep.tile([P, N, PACK], BF16, name="w_woven", tag="slot1", align_bytes=64)
        nc.vector.tensor_copy(
            out=w_woven[:].rearrange("p (c i) j -> p c j i", i=4),
            in_=w_raw[:].rearrange("p j (c i) -> p c j i", i=4),
        )
        w_codes = keep.tile([P, N], U32, name="w_codes", align_bytes=64)
        w_scales = keep.tile([P, N], U8, name="w_scales", align_bytes=64)
        nc.vector.quantize_mx(
            out=w_codes[:].bitcast(FP8X4), scales=w_scales[:], in_=w_woven[:].rearrange("p m j -> p (m j)")
        )

        x_codes = [keep.tile([P, HALF], U32, name=f"x_codes{h}", tag=f"slot{h}", align_bytes=64) for h in range(2)]
        x_scales = [keep.tile([P, HALF], U8, name=f"x_scales{h}", align_bytes=64) for h in range(2)]
        FIRST = 128
        scores = [psum.tile([P, w], F32, name=f"scores{b}") for b, w in enumerate((FIRST, S - FIRST))]
        pieces = (
            ((0, FIRST, scores[0][:]), (FIRST, HALF, scores[1][:, : HALF - FIRST])),
            ((0, HALF, scores[1][:, HALF - FIRST :]),),
        )
        for h in range(2):
            nc.vector.quantize_mx(
                out=x_codes[h][:].bitcast(FP8X4),
                scales=x_scales[h][:],
                in_=woven_flat[:, h * HALF * PACK : (h + 1) * HALF * PACK],
            )
            for lo, hi, dst in pieces[h]:
                nc.tensor.matmul_mx(
                    out=dst,
                    lhsT=w_codes[:].bitcast(FP8X4),
                    lhsT_scale=w_scales[:],
                    rhs=x_codes[h][:, lo:hi].bitcast(FP8X4),
                    rhs_scale=x_scales[h][:, lo:hi],
                    start=True,
                    stop=True,
                )

        neg_scores = keep.tile([P, S], F32, name="neg_scores")
        neg_max = [keep.tile([P, 1], F32, name=f"neg_max{h}") for h in range(2)]
        for h, cols in enumerate((slice(0, FIRST), slice(FIRST, S))):
            nc.vector.tensor_scalar(
                out=neg_scores[:, cols],
                in0=scores[h][:],
                scalar1=-1.0,
                scalar2=(neg_max[0][:] if h else None),
                op0=ALU.mult,
                op1=ALU.min,
                accum_out=neg_max[h][:],
            )

        exps = keep.tile([P, S], F32, name="exps")
        total = keep.tile([P, 1], F32, name="total")
        nc.scalar.activation(
            out=exps[:], in_=neg_scores[:], func=ACT.Exp, bias=neg_max[1][:], scale=-1.0, accum_out=total[:]
        )
        inv_total = keep.tile([P, 1], F32, name="inv_total")
        nc.vector.reciprocal(out=inv_total[:], in_=total[:])
        result = [keep.tile([P, HALF], F32, name=f"result{h}") for h in range(2)]
        for h, queue in enumerate((nc.sync, nc.scalar)):
            cols = slice(h * HALF, (h + 1) * HALF)
            nc.vector.tensor_scalar(
                out=result[h][:], in0=exps[:, cols], scalar1=inv_total[:], scalar2=None, op0=ALU.mult
            )
            queue.dma_start(out=out[:, cols], in_=result[h][:])
